import numpy as np
import ml_dtypes


def mxq(x, axis, fmt="e4m3"):
    dtype, down = {"e4m3": (ml_dtypes.float8_e4m3fn, 7), "e5m2": (ml_dtypes.float8_e5m2, 14)}[fmt]
    v = np.moveaxis(np.asarray(x, np.float32).astype(ml_dtypes.bfloat16).astype(np.float64), axis, -1)
    blocks = v.reshape(v.shape[:-1] + (-1, 32))
    amax = np.abs(blocks).max(-1, keepdims=True)
    byte = np.maximum(np.where(amax > 0, np.frexp(amax)[1] - 1 + 127, 0) - down, 1)
    scale = np.exp2(byte - 127.0)
    codes = (blocks / scale).astype(np.float32).astype(dtype).astype(np.float64)
    return np.moveaxis((codes * scale).reshape(v.shape), -1, axis)


WIDE = False


def mx_kscale(k):
    if not WIDE:
        return np.ones(k)
    levels = np.array([30, -30])
    if k % 512:
        return np.exp2(np.random.permutation(np.resize(levels, k // 32))).repeat(32)
    a = np.empty((k // 512, 16))
    for p in range(k // 512):
        a[p, :8] = np.random.permutation(np.resize(levels, 8))
        for g in range(8):
            far = levels[np.abs(levels - a[p, g]) >= 10]
            a[p, g + 8] = far[np.random.randint(len(far))]
    return np.exp2(a.ravel()).repeat(32)


def f64(x):
    return np.asarray(x).astype(np.float64)


K, M, T = 1536, 512, 512


def setup_inputs():
    n = np.random.standard_normal
    s1 = mx_kscale(K)[:, None]
    s2 = mx_kscale(K)[:, None]
    return {
        "w": (n((K, M)) / np.sqrt(K) * s1).astype(np.float32),
        "xd": (n((K, T)) / s1).astype(np.float32),
        "wd": (n((K, M)) / np.sqrt(K) * s2).astype(np.float32),
        "x": (n((K, T)) / s2).astype(np.float32),
        "g": (n((512, 512))).astype(np.float32),
    }


def reference(w, xd, wd, x, g):
    w_ = mxq(f64(w), 0, "e4m3")
    xd_ = mxq(f64(xd), 0, "e5m2")
    wd_ = mxq(f64(wd), 0, "e5m2")
    x_ = mxq(f64(x), 0, "e4m3")
    y = xd_.T @ w_ + x_.T @ wd_
    return f64(g) * y

@@ -1,0 +1,120 @@
+from contextlib import ExitStack
+
+import concourse.mybir as mybir
+
+K, M, T = 1536, 512, 512
+
+FLOPS = 2 * 2 * K * M * T
+
+F32 = mybir.dt.float32
+BF16 = mybir.dt.bfloat16
+U32 = mybir.dt.uint32
+U8 = mybir.dt.uint8
+E4M3 = mybir.dt.float8_e4m3fn_x4
+E5M2 = mybir.dt.float8_e5m2_x4
+
+P = 128
+PACK = 4
+K_PASS = P * PACK
+PASSES = K // K_PASS
+TILES = T // P
+V_COLS = 256
+
+
+def interleaved(tile, cols):
+    return tile[:, 0 : PACK * cols].rearrange("p (c i j) -> p c j i", i=4, j=PACK)
+
+
+def grouped_source(raw, c0, c1):
+    return raw[:, :, c0:c1].rearrange("p j (c i) -> p c j i", i=4)
+
+
+def tile_mix_jvp_tm_mul_kernel(tc, w, xd, wd, x, g, out):
+    nc = tc.nc
+
+    with ExitStack() as ctx:
+        raws = ctx.enter_context(tc.tile_pool(name="raws", bufs=1))
+        stage = ctx.enter_context(tc.tile_pool(name="stage", bufs=4))
+        keep = ctx.enter_context(tc.tile_pool(name="keep", bufs=1))
+        psum = ctx.enter_context(tc.psum_pool(name="psum", bufs=1))
+        ctx.enter_context(tc.manual_schedule())
+
+        order = [("w", w, E4M3), ("wd", wd, E5M2), ("xd", xd, E5M2), ("x", x, E4M3)]
+
+        raw = {}
+        for name, src, fmt in order:
+            for c in range(PASSES):
+                r = raws.tile([P, PACK, T], F32, name="raw_%s%d" % (name, c), align_bytes=64)
+                rows = src[c * K_PASS : (c + 1) * K_PASS, :]
+                nc.sync.dma_start(out=r[:], in_=rows.rearrange("(p j) w -> p j w", j=PACK))
+                raw[name, c] = r
+        gs = []
+        for i in range(TILES):
+            gt = keep.tile([P, M], F32, name="g%d" % i, align_bytes=64)
+            nc.sync.dma_start(out=gt[:], in_=g[i * P : (i + 1) * P, :])
+            gs.append(gt)
+
+        acc = [psum.tile([P, M], F32, name="acc%d" % i) for i in range(TILES)]
+
+        codes = {}
+        scales = {}
+
+        def multiply(name, c, i, lhs, lhs_scale):
+            wname, lfmt, rfmt = ("w", E5M2, E4M3) if name == "xd" else ("wd", E4M3, E5M2)
+            nc.tensor.matmul_mx(
+                out=acc[i][:],
+                lhsT=lhs.bitcast(lfmt),
+                lhsT_scale=lhs_scale,
+                rhs=codes[wname, c][:].bitcast(rfmt),
+                rhs_scale=scales[wname, c][:],
+                start=(name == "xd" and c == 0),
+                stop=(name == "x" and c == PASSES - 1),
+            )
+
+        for name, src, fmt in order:
+            for c in range(PASSES):
+                if name == "x" and c == PASSES - 1:
+                    continue
+                r = raw[name, c]
+                grp = stage.tile([P, PACK * T], BF16, name="grp", align_bytes=64)
+                nc.vector.tensor_copy(out=interleaved(grp[:, 0 : PACK * V_COLS], V_COLS), in_=grouped_source(r, 0, V_COLS))
+                nc.scalar.copy(out=interleaved(grp[:, PACK * V_COLS : PACK * T], T - V_COLS), in_=grouped_source(r, V_COLS, T))
+                cd = keep.tile([P, T], U32, name="codes_%s%d" % (name, c), align_bytes=64)
+                sc = keep.tile([P, T], U8, name="scales_%s%d" % (name, c), align_bytes=64)
+                nc.vector.quantize_mx(out=cd[:].bitcast(fmt), scales=sc[:], in_=grp[:])
+                codes[name, c] = cd
+                scales[name, c] = sc
+                if name in ("xd", "x"):
+                    for i in range(TILES):
+                        cols = slice(i * P, (i + 1) * P)
+                        multiply(name, c, i, cd[:, cols], sc[:, cols])
+
+        last = PASSES - 1
+        r = raw["x", last]
+        grps = [stage.tile([P, PACK * P], BF16, name="grp_last%d" % i, align_bytes=64) for i in range(TILES)]
+        for i in range(TILES):
+            copy = nc.vector.tensor_copy if i == 0 else nc.scalar.copy
+            copy(out=interleaved(grps[i], P), in_=grouped_source(r, i * P, (i + 1) * P))
+
+        def quantise_last(i):
+            cd = keep.tile([P, P], U32, name="codes_last%d" % i, align_bytes=64)
+            sc = keep.tile([P, P], U8, name="scales_last%d" % i, align_bytes=64)
+            nc.vector.quantize_mx(out=cd[:].bitcast(E4M3), scales=sc[:], in_=grps[i][:])
+            multiply("x", last, i, cd[:], sc[:])
+
+        def finish(i, pieces):
+            width = M // pieces
+            for h in range(pieces):
+                cols = slice(h * width, (h + 1) * width)
+                res = keep.tile([P, width], F32, name="res%d_%d" % (i, h), align_bytes=64)
+                nc.vector.tensor_mul(out=res[:], in0=acc[i][:, cols], in1=gs[i][:, cols])
+                nc.sync.dma_start(out=out[i * P : (i + 1) * P, cols], in_=res[:])
+
+        quantise_last(0)
+        quantise_last(1)
+        finish(0, 1)
+        quantise_last(2)
+        finish(1, 1)
+        quantise_last(3)
+        finish(2, 1)
+        finish(3, 2)

@@ -18,15 +18,15 @@ PACK = 4
 K_PASS = P * PACK
 PASSES = K // K_PASS
 TILES = T // P
-V_COLS = 256
+HALF = T // 2
 
 
-def interleaved(tile, cols):
-    return tile[:, 0 : PACK * cols].rearrange("p (c i j) -> p c j i", i=4, j=PACK)
-
-
-def grouped_source(raw, c0, c1):
-    return raw[:, :, c0:c1].rearrange("p j (c i) -> p c j i", i=4)
+def round_and_interleave(copy, grp, raw, c0, c1, j0=0):
+    dst = grp[:, PACK * c0 : PACK * c1].rearrange("p (c i j) -> p c j i", i=4, j=PACK)
+    copy(
+        out=dst[:, :, j0 : j0 + raw.shape[1], :],
+        in_=raw[:, :, c0:c1].rearrange("p j (c i) -> p c j i", i=4),
+    )
 
 
 def tile_mix_jvp_tm_mul_kernel(tc, w, xd, wd, x, g, out):
@@ -39,15 +39,25 @@ def tile_mix_jvp_tm_mul_kernel(tc, w, xd, wd, x, g, out):
         psum = ctx.enter_context(tc.psum_pool(name="psum", bufs=1))
         ctx.enter_context(tc.manual_schedule())
 
-        order = [("w", w, E4M3), ("wd", wd, E5M2), ("xd", xd, E5M2), ("x", x, E4M3)]
+        def load(name, src, c, c0, c1):
+            r = raws.tile([P, PACK, c1 - c0], F32, name="raw_%s%d_%d" % (name, c, c0), align_bytes=64)
+            rows = src[c * K_PASS : (c + 1) * K_PASS, c0:c1]
+            nc.sync.dma_start(out=r[:], in_=rows.rearrange("(p j) w -> p j w", j=PACK))
+            return r
 
         raw = {}
-        for name, src, fmt in order:
+        for name, src in (("w", w), ("wd", wd), ("xd", xd)):
             for c in range(PASSES):
-                r = raws.tile([P, PACK, T], F32, name="raw_%s%d" % (name, c), align_bytes=64)
-                rows = src[c * K_PASS : (c + 1) * K_PASS, :]
-                nc.sync.dma_start(out=r[:], in_=rows.rearrange("(p j) w -> p j w", j=PACK))
-                raw[name, c] = r
+                raw[name, c] = load(name, src, c, 0, T)
+        raw["x", 0] = load("x", x, 0, 0, T)
+        raw_x2a = load("x", x, 2, 0, HALF)
+        raw_x1 = []
+        rows = x[K_PASS : 2 * K_PASS, :].rearrange("(p j) w -> p j w", j=PACK)
+        for h in range(2):
+            r = raws.tile([P, 2, T], F32, name="raw_x1_%d" % h, align_bytes=64)
+            nc.sync.dma_start(out=r[:], in_=rows[:, 2 * h : 2 * h + 2, :])
+            raw_x1.append(r)
+        raw_x2b = load("x", x, 2, HALF, T)
         gs = []
         for i in range(TILES):
             gt = keep.tile([P, M], F32, name="g%d" % i, align_bytes=64)
@@ -56,51 +66,66 @@ def tile_mix_jvp_tm_mul_kernel(tc, w, xd, wd, x, g, out):
 
         acc = [psum.tile([P, M], F32, name="acc%d" % i) for i in range(TILES)]
 
-        codes = {}
-        scales = {}
+        def quantise(name, grp, c0, c1, fmt):
+            width = c1 - c0
+            cd = keep.tile([P, width], U32, name="codes_%s" % name, align_bytes=64)
+            sc = keep.tile([P, width], U8, name="scales_%s" % name, align_bytes=64)
+            nc.vector.quantize_mx(out=cd[:].bitcast(fmt), scales=sc[:], in_=grp[:, PACK * c0 : PACK * c1])
+            return cd, sc
 
-        def multiply(name, c, i, lhs, lhs_scale):
+        moving = {}
+
+        def multiply(name, c, i, operand, c0, start=False, stop=False):
             wname, lfmt, rfmt = ("w", E5M2, E4M3) if name == "xd" else ("wd", E4M3, E5M2)
+            cols = slice(i * P - c0, (i + 1) * P - c0)
             nc.tensor.matmul_mx(
                 out=acc[i][:],
-                lhsT=lhs.bitcast(lfmt),
-                lhsT_scale=lhs_scale,
-                rhs=codes[wname, c][:].bitcast(rfmt),
-                rhs_scale=scales[wname, c][:],
-                start=(name == "xd" and c == 0),
-                stop=(name == "x" and c == PASSES - 1),
+                lhsT=operand[0][:, cols].bitcast(lfmt),
+                lhsT_scale=operand[1][:, cols],
+                rhs=moving[wname, c][0][:].bitcast(rfmt),
+                rhs_scale=moving[wname, c][1][:],
+                start=start,
+                stop=stop,
             )
 
-        for name, src, fmt in order:
-            for c in range(PASSES):
-                if name == "x" and c == PASSES - 1:
-                    continue
-                r = raw[name, c]
+        for name, fmt in (("w", E4M3), ("wd", E5M2), ("xd", E5M2), ("x", E4M3)):
+            for c in range(1 if name == "x" else PASSES):
                 grp = stage.tile([P, PACK * T], BF16, name="grp", align_bytes=64)
-                nc.vector.tensor_copy(out=interleaved(grp[:, 0 : PACK * V_COLS], V_COLS), in_=grouped_source(r, 0, V_COLS))
-                nc.scalar.copy(out=interleaved(grp[:, PACK * V_COLS : PACK * T], T - V_COLS), in_=grouped_source(r, V_COLS, T))
-                cd = keep.tile([P, T], U32, name="codes_%s%d" % (name, c), align_bytes=64)
-                sc = keep.tile([P, T], U8, name="scales_%s%d" % (name, c), align_bytes=64)
-                nc.vector.quantize_mx(out=cd[:].bitcast(fmt), scales=sc[:], in_=grp[:])
-                codes[name, c] = cd
-                scales[name, c] = sc
-                if name in ("xd", "x"):
+                round_and_interleave(nc.vector.tensor_copy, grp, raw[name, c], 0, HALF)
+                round_and_interleave(nc.scalar.copy, grp, raw[name, c], HALF, T)
+                operand = quantise("%s%d" % (name, c), grp, 0, T, fmt)
+                if name in ("w", "wd"):
+                    moving[name, c] = operand
+                else:
                     for i in range(TILES):
-                        cols = slice(i * P, (i + 1) * P)
-                        multiply(name, c, i, cd[:, cols], sc[:, cols])
+                        multiply(name, c, i, operand, 0, start=(name == "xd" and c == 0))
 
-        last = PASSES - 1
-        r = raw["x", last]
-        grps = [stage.tile([P, PACK * P], BF16, name="grp_last%d" % i, align_bytes=64) for i in range(TILES)]
-        for i in range(TILES):
-            copy = nc.vector.tensor_copy if i == 0 else nc.scalar.copy
-            copy(out=interleaved(grps[i], P), in_=grouped_source(r, i * P, (i + 1) * P))
+        grp = stage.tile([P, PACK * HALF], BF16, name="grp_x2a", align_bytes=64)
+        round_and_interleave(nc.vector.tensor_copy, grp, raw_x2a, 0, P)
+        round_and_interleave(nc.scalar.copy, grp, raw_x2a, P, HALF)
+        operand = quantise("x2a", grp, 0, HALF, E4M3)
+        for i in (0, 1):
+            multiply("x", 2, i, operand, 0)
 
-        def quantise_last(i):
-            cd = keep.tile([P, P], U32, name="codes_last%d" % i, align_bytes=64)
-            sc = keep.tile([P, P], U8, name="scales_last%d" % i, align_bytes=64)
-            nc.vector.quantize_mx(out=cd[:].bitcast(E4M3), scales=sc[:], in_=grps[i][:])
-            multiply("x", last, i, cd[:], sc[:])
+        grp = stage.tile([P, PACK * T], BF16, name="grp", align_bytes=64)
+        for h in range(2):
+            round_and_interleave(nc.vector.tensor_copy, grp, raw_x1[h], 0, HALF, 2 * h)
+            round_and_interleave(nc.scalar.copy, grp, raw_x1[h], HALF, T, 2 * h)
+        for i in (0, 1):
+            operand = quantise("x1_%d" % i, grp, i * P, (i + 1) * P, E4M3)
+            multiply("x", 1, i, operand, i * P, stop=True)
+        operand = quantise("x1b", grp, HALF, T, E4M3)
+        for i in (2, 3):
+            multiply("x", 1, i, operand, HALF)
+
+        grp_x2b = stage.tile([P, PACK * HALF], BF16, name="grp_x2b", align_bytes=64)
+        round_and_interleave(nc.scalar.copy, grp_x2b, raw_x2b, 0, P)
+        round_and_interleave(nc.scalar.copy, grp_x2b, raw_x2b, P + 64, HALF)
+        round_and_interleave(nc.vector.tensor_copy, grp_x2b, raw_x2b, P, P + 64)
+
+        def last_product(i):
+            operand = quantise("x2b%d" % i, grp_x2b, (i - 2) * P, (i - 1) * P, E4M3)
+            multiply("x", 2, i, operand, i * P, stop=True)
 
         def finish(i, pieces):
             width = M // pieces
@@ -110,11 +135,9 @@ def tile_mix_jvp_tm_mul_kernel(tc, w, xd, wd, x, g, out):
                 nc.vector.tensor_mul(out=res[:], in0=acc[i][:, cols], in1=gs[i][:, cols])
                 nc.sync.dma_start(out=out[i * P : (i + 1) * P, cols], in_=res[:])
 
-        quantise_last(0)
-        quantise_last(1)
-        finish(0, 1)
-        quantise_last(2)
+        last_product(2)
+        finish(0, 2)
+        last_product(3)
         finish(1, 1)
-        quantise_last(3)
         finish(2, 1)
         finish(3, 2)

from contextlib import ExitStack

import concourse.mybir as mybir

K, M, T = 1536, 512, 512

FLOPS = 2 * 2 * K * M * T

F32 = mybir.dt.float32
BF16 = mybir.dt.bfloat16
U32 = mybir.dt.uint32
U8 = mybir.dt.uint8
E4M3 = mybir.dt.float8_e4m3fn_x4
E5M2 = mybir.dt.float8_e5m2_x4

P = 128
PACK = 4
K_PASS = P * PACK
PASSES = K // K_PASS
TILES = T // P
HALF = T // 2


def round_and_interleave(copy, grp, raw, c0, c1, j0=0):
    dst = grp[:, PACK * c0 : PACK * c1].rearrange("p (c i j) -> p c j i", i=4, j=PACK)
    copy(
        out=dst[:, :, j0 : j0 + raw.shape[1], :],
        in_=raw[:, :, c0:c1].rearrange("p j (c i) -> p c j i", i=4),
    )


def tile_mix_jvp_tm_mul_kernel(tc, w, xd, wd, x, g, out):
    nc = tc.nc

    with ExitStack() as ctx:
        raws = ctx.enter_context(tc.tile_pool(name="raws", bufs=1))
        stage = ctx.enter_context(tc.tile_pool(name="stage", bufs=4))
        keep = ctx.enter_context(tc.tile_pool(name="keep", bufs=1))
        psum = ctx.enter_context(tc.psum_pool(name="psum", bufs=1))
        ctx.enter_context(tc.manual_schedule())

        def load(name, src, c, c0, c1):
            r = raws.tile([P, PACK, c1 - c0], F32, name="raw_%s%d_%d" % (name, c, c0), align_bytes=64)
            rows = src[c * K_PASS : (c + 1) * K_PASS, c0:c1]
            nc.sync.dma_start(out=r[:], in_=rows.rearrange("(p j) w -> p j w", j=PACK))
            return r

        raw = {}
        for name, src in (("w", w), ("wd", wd), ("xd", xd)):
            for c in range(PASSES):
                raw[name, c] = load(name, src, c, 0, T)
        raw["x", 0] = load("x", x, 0, 0, T)
        raw_x2a = load("x", x, 2, 0, HALF)
        raw_x1 = []
        rows = x[K_PASS : 2 * K_PASS, :].rearrange("(p j) w -> p j w", j=PACK)
        for h in range(2):
            r = raws.tile([P, 2, T], F32, name="raw_x1_%d" % h, align_bytes=64)
            nc.sync.dma_start(out=r[:], in_=rows[:, 2 * h : 2 * h + 2, :])
            raw_x1.append(r)
        raw_x2b = load("x", x, 2, HALF, T)
        gs = []
        for i in range(TILES):
            gt = keep.tile([P, M], F32, name="g%d" % i, align_bytes=64)
            nc.sync.dma_start(out=gt[:], in_=g[i * P : (i + 1) * P, :])
            gs.append(gt)

        acc = [psum.tile([P, M], F32, name="acc%d" % i) for i in range(TILES)]

        def quantise(name, grp, c0, c1, fmt):
            width = c1 - c0
            cd = keep.tile([P, width], U32, name="codes_%s" % name, align_bytes=64)
            sc = keep.tile([P, width], U8, name="scales_%s" % name, align_bytes=64)
            nc.vector.quantize_mx(out=cd[:].bitcast(fmt), scales=sc[:], in_=grp[:, PACK * c0 : PACK * c1])
            return cd, sc

        moving = {}

        def multiply(name, c, i, operand, c0, start=False, stop=False):
            wname, lfmt, rfmt = ("w", E5M2, E4M3) if name == "xd" else ("wd", E4M3, E5M2)
            cols = slice(i * P - c0, (i + 1) * P - c0)
            nc.tensor.matmul_mx(
                out=acc[i][:],
                lhsT=operand[0][:, cols].bitcast(lfmt),
                lhsT_scale=operand[1][:, cols],
                rhs=moving[wname, c][0][:].bitcast(rfmt),
                rhs_scale=moving[wname, c][1][:],
                start=start,
                stop=stop,
            )

        for name, fmt in (("w", E4M3), ("wd", E5M2), ("xd", E5M2), ("x", E4M3)):
            for c in range(1 if name == "x" else PASSES):
                grp = stage.tile([P, PACK * T], BF16, name="grp", align_bytes=64)
                round_and_interleave(nc.vector.tensor_copy, grp, raw[name, c], 0, HALF)
                round_and_interleave(nc.scalar.copy, grp, raw[name, c], HALF, T)
                operand = quantise("%s%d" % (name, c), grp, 0, T, fmt)
                if name in ("w", "wd"):
                    moving[name, c] = operand
                else:
                    for i in range(TILES):
                        multiply(name, c, i, operand, 0, start=(name == "xd" and c == 0))

        grp = stage.tile([P, PACK * HALF], BF16, name="grp_x2a", align_bytes=64)
        round_and_interleave(nc.vector.tensor_copy, grp, raw_x2a, 0, P)
        round_and_interleave(nc.scalar.copy, grp, raw_x2a, P, HALF)
        operand = quantise("x2a", grp, 0, HALF, E4M3)
        for i in (0, 1):
            multiply("x", 2, i, operand, 0)

        grp = stage.tile([P, PACK * T], BF16, name="grp", align_bytes=64)
        for h in range(2):
            round_and_interleave(nc.vector.tensor_copy, grp, raw_x1[h], 0, HALF, 2 * h)
            round_and_interleave(nc.scalar.copy, grp, raw_x1[h], HALF, T, 2 * h)
        for i in (0, 1):
            operand = quantise("x1_%d" % i, grp, i * P, (i + 1) * P, E4M3)
            multiply("x", 1, i, operand, i * P, stop=True)
        operand = quantise("x1b", grp, HALF, T, E4M3)
        for i in (2, 3):
            multiply("x", 1, i, operand, HALF)

        grp_x2b = stage.tile([P, PACK * HALF], BF16, name="grp_x2b", align_bytes=64)
        round_and_interleave(nc.scalar.copy, grp_x2b, raw_x2b, 0, P)
        round_and_interleave(nc.scalar.copy, grp_x2b, raw_x2b, P + 64, HALF)
        round_and_interleave(nc.vector.tensor_copy, grp_x2b, raw_x2b, P, P + 64)

        def last_product(i):
            operand = quantise("x2b%d" % i, grp_x2b, (i - 2) * P, (i - 1) * P, E4M3)
            multiply("x", 2, i, operand, i * P, stop=True)

        def finish(i, pieces):
            width = M // pieces
            for h in range(pieces):
                cols = slice(h * width, (h + 1) * width)
                res = keep.tile([P, width], F32, name="res%d_%d" % (i, h), align_bytes=64)
                nc.vector.tensor_mul(out=res[:], in0=acc[i][:, cols], in1=gs[i][:, cols])
                nc.sync.dma_start(out=out[i * P : (i + 1) * P, cols], in_=res[:])

        last_product(2)
        finish(0, 2)
        last_product(3)
        finish(1, 1)
        finish(2, 1)
        finish(3, 2)
